import numpy as np
import ml_dtypes


def mxq(x, axis, fmt="e4m3"):
    dtype, down = {"e4m3": (ml_dtypes.float8_e4m3fn, 7), "e5m2": (ml_dtypes.float8_e5m2, 14)}[fmt]
    v = np.moveaxis(np.asarray(x, np.float32).astype(ml_dtypes.bfloat16).astype(np.float64), axis, -1)
    blocks = v.reshape(v.shape[:-1] + (-1, 32))
    amax = np.abs(blocks).max(-1, keepdims=True)
    byte = np.maximum(np.where(amax > 0, np.frexp(amax)[1] - 1 + 127, 0) - down, 1)
    scale = np.exp2(byte - 127.0)
    codes = (blocks / scale).astype(np.float32).astype(dtype).astype(np.float64)
    return np.moveaxis((codes * scale).reshape(v.shape), -1, axis)


WIDE = False


def mx_kscale(k):
    if not WIDE:
        return np.ones(k)
    levels = np.array([10, -10, 5, -5, 0])
    if k % 512:
        return np.exp2(np.random.permutation(np.resize(levels, k // 32))).repeat(32)
    a = np.empty((k // 512, 16))
    for p in range(k // 512):
        a[p, :8] = np.random.permutation(np.resize(levels, 8))
        for g in range(8):
            far = levels[np.abs(levels - a[p, g]) >= 10]
            a[p, g + 8] = far[np.random.randint(len(far))]
    return np.exp2(a.ravel()).repeat(32)


def f64(x):
    return np.asarray(x).astype(np.float64)


def striped(idx):
    return np.tile(idx.reshape(-1, 16).T, (8, 1)).astype(np.uint16)


def unstriped(offs):
    return offs[:16].T.reshape(-1).astype(np.int64)


E2M1 = np.array([0.0, 0.5, 1.0, 1.5, 2.0, 3.0, 4.0, 6.0, -0.0, -0.5, -1.0, -1.5, -2.0, -3.0, -4.0, -6.0])


def pack_weight(w, fmt):
    k, n = w.shape
    w = f64(np.asarray(w, np.float32).astype(ml_dtypes.bfloat16)).reshape(k // 32, 32, n)
    amax = np.abs(w).max(1)
    if fmt == "e4m3":
        byte = np.frexp(amax)[1] - 1 + 127 - 7
    else:
        mant, ex = np.frexp(amax / 6.0)
        byte = np.where(mant > 0.5, ex, ex - 1) + 127
    byte = np.clip(np.where(amax > 0, byte, 1), 1, 254)
    scaled = (w * np.exp2(127.0 - byte)[:, None, :]).reshape(k, n).astype(np.float32)
    by_word = np.ascontiguousarray(scaled.reshape(k // 512, 128, 4, n).transpose(0, 1, 3, 2))
    if fmt == "e4m3":
        words = by_word.astype(ml_dtypes.float8_e4m3fn).view(np.uint8)
    else:
        c = by_word.astype(ml_dtypes.float4_e2m1fn).view(np.uint8) & 0xF
        words = (c[..., 0::2] | (c[..., 1::2] << 4)).reshape(k // 512, 128, 2 * n)
    return np.ascontiguousarray(words), np.ascontiguousarray(byte.astype(np.uint8).reshape(k // 512, 16, n))


def unpack_weight(words, scales, fmt):
    g, _, n = scales.shape
    words = np.ascontiguousarray(words).reshape(g, 128, n, -1)
    if fmt == "e4m3":
        vals = words.view(ml_dtypes.float8_e4m3fn).astype(np.float64)
    else:
        nib = np.empty((g, 128, n, 4), np.uint8)
        nib[..., 0::2] = words & 0xF
        nib[..., 1::2] = words >> 4
        vals = E2M1[nib]
    vals = vals * np.repeat(np.exp2(scales.astype(np.float64) - 127.0), 8, axis=1)[..., None]
    return vals.transpose(0, 1, 3, 2).reshape(g * 512, n)


def gelu(v):
    return 0.5 * v * (1.0 + np.tanh(np.sqrt(2.0 / np.pi) * (v + 0.044715 * v**3)))


def bf(x):
    return np.asarray(x, np.float32).astype(ml_dtypes.bfloat16)


def planes(Y):
    n, m = Y.shape
    b = f64(bf(Y)).reshape(n // 32, 32, m)
    amax = np.abs(b).max(1)
    byte = np.clip(np.where(amax > 0, np.frexp(amax)[1] - 1 + 127 - 7, 1), 1, 254)
    codes = (b * np.exp2(127.0 - byte)[:, None, :]).reshape(n, m).astype(np.float32).astype(ml_dtypes.float8_e4m3fn).view(np.uint8)
    words = codes.reshape(n // 512, 128, 4, m).transpose(0, 1, 3, 2)
    return np.ascontiguousarray(words), np.ascontiguousarray(byte.astype(np.uint8).reshape(n // 512, 16, m))


K, H, N, T, S, P, P2 = 1024, 512, 1024, 4096, 2048, 1024, 512

def setup_inputs():
    n = np.random.standard_normal
    s = mx_kscale(K)[:, None]
    u = mx_kscale(H)[:, None]
    tab_words, tab_scales = pack_weight(n((K, T)) * s, "e4m3")
    w4_words, w4_scales = pack_weight(n((K, H)) / np.sqrt(K) / s * u.T, "e2m1")
    w2 = n((H, N)) / np.sqrt(H) / u * np.exp(0.8 * n(N))[None, :]
    return {
        "tab_words": tab_words, "tab_scales": tab_scales,
        "offs": striped(np.random.permutation(T)[:S]),
        "pos1": striped(np.random.permutation(S)[:P]),
        "pos2": striped(np.random.permutation(S)[:P]),
        "pos3": striped(np.random.permutation(P)[:P2]),
        "pos4": striped(np.random.permutation(S)[:P2]),
        "w4_words": w4_words, "w4_scales": w4_scales,
        "gm": np.exp(0.5 * n((H, S))).astype(np.float32),
        "d": (0.7 * n(H) * u[:, 0]).astype(np.float32),
        "sv": (np.exp(0.3 * n(H)) / u[:, 0]).astype(np.float32),
        "w2": w2.astype(np.float32),
    }

def reference(tab_words, tab_scales, offs, pos1, pos2, pos3, pos4, w4_words, w4_scales, gm, d, sv, w2):
    v = unpack_weight(tab_words, tab_scales, "e4m3")[:, unstriped(offs)]
    w4 = unpack_weight(w4_words, w4_scales, "e2m1")
    h = (w4.T @ v) * f64(gm)
    a1 = np.maximum(h[:, unstriped(pos1)], h[:, unstriped(pos2)]) + f64(d)[:, None]
    listing = np.tanh(f64(sv)[:, None] * h[:, unstriped(pos4)])
    a2 = a1[:, unstriped(pos3)] * listing
    y = mxq(f64(w2), 0, "e4m3").T @ mxq(a2, 0, "e4m3")
    words, scales = planes(y)
    return y, words, scales

@@ -1,0 +1,242 @@
+from contextlib import ExitStack
+
+import concourse.mybir as mybir
+
+K, H, N, T, S, PAIRS, KEPT = 1024, 512, 1024, 4096, 2048, 1024, 512
+FLOPS = 2 * (K * H * S + H * N * KEPT)
+
+F32 = mybir.dt.float32
+BF16 = mybir.dt.bfloat16
+I32 = mybir.dt.int32
+U32 = mybir.dt.uint32
+U16 = mybir.dt.uint16
+U8 = mybir.dt.uint8
+FP8X4 = mybir.dt.float8_e4m3fn_x4
+FP4X4 = mybir.dt.float4_e2m1fn_x4
+ALU = mybir.AluOpType
+ACT = mybir.ActivationFunctionType
+
+P = 128
+PACK = 4
+PASSES = K // (P * PACK)
+GROUPS = N // (P * PACK)
+CHUNK = 512
+CHUNKS = S // CHUNK
+BLOCK = 128
+BLOCKS = KEPT // BLOCK
+QUAD = 32
+PARKED = QUAD - PASSES * PACK
+SPAN = 3 * QUAD + PACK
+
+
+def tile_list_stolen_view_features_kernel(
+    tc, tab_words, tab_scales, offs, pos1, pos2, pos3, pos4, w4_words, w4_scales, gm, d, sv, w2, out_0, out_1, out_2
+):
+    nc = tc.nc
+    with ExitStack() as ctx:
+        lists = ctx.enter_context(tc.tile_pool(name="lists", bufs=1))
+        keep = ctx.enter_context(tc.tile_pool(name="keep", bufs=1))
+        ring2 = ctx.enter_context(tc.tile_pool(name="ring2", bufs=2))
+        ring3 = ctx.enter_context(tc.tile_pool(name="ring3", bufs=3))
+        psum = ctx.enter_context(tc.psum_pool(name="psum", bufs=8))
+
+        def load_list(src, name):
+            held = lists.tile(list(src.shape), U16, name=name)
+            nc.sync.dma_start(held[:], src)
+            return held
+
+        idx = load_list(offs, "idx")
+        table_scales = keep.tile([P, T], U8, align_bytes=64)
+        for q in range(4):
+            nc.sync.dma_start(
+                out=table_scales[QUAD * q + PARKED : QUAD * (q + 1), :].bitcast(I32),
+                in_=tab_scales[:, PACK * q : PACK * (q + 1), :].bitcast(I32),
+            )
+        for q in range(4):
+            eng = nc.vector if q % 2 == 0 else nc.gpsimd
+            eng.memset(table_scales[QUAD * q : QUAD * q + PARKED, :].bitcast(I32), 0)
+
+        table_words = [keep.tile([P, T], U32, name=f"table_words{a}", align_bytes=64) for a in range(PASSES)]
+
+        def load_table_words(a):
+            nc.sync.dma_start(
+                out=table_words[a][:].bitcast(I32), in_=tab_words[a].rearrange("p n t -> p (n t)").bitcast(I32)
+            )
+
+        load_table_words(0)
+        p1 = load_list(pos1, "p1")
+        p2 = load_list(pos2, "p2")
+        p4 = load_list(pos4, "p4")
+        p3 = load_list(pos3, "p3")
+        w4_raw = keep.tile([P, PASSES, 2 * H], U8, align_bytes=64)
+        nc.sync.dma_start(out=w4_raw[:].bitcast(I32), in_=w4_words.rearrange("a p c -> p a c").bitcast(I32))
+        load_table_words(1)
+        gm_rows = gm.rearrange("(p t) j -> p t j", t=PACK)
+        gains = [keep.tile([P, S], F32, name=f"gains{t}") for t in range(PACK)]
+        for t in range(PACK):
+            nc.sync.dma_start(out=gains[t][:], in_=gm_rows[:, t, :])
+        w2_raw = keep.tile([P, PACK, N], F32)
+        nc.sync.dma_start(out=w2_raw[:], in_=w2.rearrange("(p j) n -> p j n", j=PACK))
+
+        w4_scales_raw = keep.tile([P, PASSES, H], U8, align_bytes=64)
+        nc.gpsimd.memset(w4_scales_raw[:].bitcast(I32), 0)
+        for q in range(4):
+            nc.gpsimd.dma_start(
+                out=w4_scales_raw[QUAD * q : QUAD * q + PACK, :, :].bitcast(I32),
+                in_=w4_scales[:, PACK * q : PACK * (q + 1), :].rearrange("a r c -> r a c").bitcast(I32),
+            )
+        shift = keep.tile([P, PACK], F32)
+        nc.gpsimd.dma_start(out=shift[:], in_=d.rearrange("(p t) -> p t", t=PACK))
+        slope = keep.tile([P, PACK], F32)
+        nc.gpsimd.dma_start(out=slope[:], in_=sv.rearrange("(p t) -> p t", t=PACK))
+
+        w4_codes = keep.tile([P, PASSES, PACK, 2 * P], U8, align_bytes=64)
+        nc.scalar.copy(
+            out=w4_codes[:].bitcast(U16),
+            in_=w4_raw[:].bitcast(U16).rearrange("p a (m t) -> p a t m", t=PACK),
+        )
+        w4_planes = keep.tile([P, PASSES, PACK, P], U8, align_bytes=64)
+        nc.gpsimd.tensor_copy(out=w4_planes[:], in_=w4_scales_raw[:].rearrange("p a (m t) -> p a t m", t=PACK))
+
+        picked_scales = keep.tile([P, S], U8, align_bytes=64)
+        nc.vector.tensor_copy(picked_scales[:], table_scales[:].indirect(idx[:]))
+        v_planes = keep.tile([P, PASSES, S], U8, align_bytes=64)
+        nc.gpsimd.memset(v_planes[:].bitcast(I32), 0)
+        for a in range(PASSES):
+            first = PARKED + PACK * a
+            nc.scalar.dma_start(
+                out=v_planes[0:SPAN, a, :].bitcast(I32), in_=picked_scales[first : first + SPAN, :].bitcast(I32)
+            )
+        v_first = keep.tile([P, S], U32, align_bytes=64)
+        nc.vector.tensor_copy(v_first[:], table_words[0][:].indirect(idx[:]))
+        v_second = [keep.tile([P, CHUNK], U32, name=f"v_second{c}", align_bytes=64) for c in range(CHUNKS)]
+        per = CHUNK // 16
+        for c in range(CHUNKS):
+            nc.vector.tensor_copy(v_second[c][:], table_words[1][:].indirect(idx[:, per * c : per * (c + 1)]))
+
+        w2_codes = keep.tile([P, GROUPS, PACK, P], U32, align_bytes=64)
+        w2_planes = keep.tile([P, GROUPS, PACK, P], U8, align_bytes=64)
+        w2_rounded = [keep.tile([P, PACK, P, PACK], BF16, name=f"w2_rounded{g}", align_bytes=64) for g in range(GROUPS)]
+
+        def round_w2(g):
+            nc.scalar.copy(
+                out=w2_rounded[g][:].rearrange("p t m j -> p m j t"),
+                in_=w2_raw[:, :, 512 * g : 512 * (g + 1)].rearrange("p j (m t) -> p m j t", t=PACK),
+            )
+
+        def quantize_w2(g):
+            nc.vector.quantize_mx(
+                out=w2_codes[:, g].rearrange("p t m -> p (t m)").bitcast(FP8X4),
+                scales=w2_planes[:, g].rearrange("p t m -> p (t m)"),
+                in_=w2_rounded[g][:].rearrange("p t m j -> p (t m j)"),
+            )
+
+        pairs = [keep.tile([P, PAIRS], F32, name=f"pairs{t}") for t in range(PACK)]
+        listing = [keep.tile([P, KEPT], F32, name=f"listing{t}") for t in range(PACK)]
+        for t in range(PACK):
+            views = ring3.tile([P, S], F32, name="views")
+            for c in range(CHUNKS):
+                cols = slice(CHUNK * c, CHUNK * (c + 1))
+                bank = psum.tile([P, CHUNK], F32, name="bank")
+                for a in range(PASSES):
+                    moving = v_first[:, cols] if a == 0 else v_second[c][:]
+                    nc.tensor.matmul_mx(
+                        out=bank[:],
+                        lhsT=w4_codes[:, a, t, :].bitcast(FP4X4),
+                        lhsT_scale=w4_planes[:, a, t, :],
+                        rhs=moving.bitcast(FP8X4),
+                        rhs_scale=v_planes[:, a, cols],
+                        start=(a == 0),
+                        stop=(a == PASSES - 1),
+                    )
+                nc.vector.tensor_tensor(views[:, cols], bank[:], gains[t][:, cols], ALU.mult)
+            left = keep.tile([P, PAIRS], F32, name="left")
+            right = keep.tile([P, PAIRS], F32, name="right")
+            nc.vector.tensor_copy(left[:], views[:].indirect(p1[:]))
+            nc.vector.tensor_copy(right[:], views[:].indirect(p2[:]))
+            listed = ring2.tile([P, KEPT], F32, name="listed")
+            nc.vector.tensor_copy(listed[:], views[:].indirect(p4[:]))
+            larger = ring2.tile([P, PAIRS], F32, name="larger")
+            nc.vector.tensor_tensor(larger[:], left[:], right[:], ALU.max)
+            nc.scalar.activation(listing[t][:], listed[:], ACT.Tanh, scale=slope[:, t : t + 1])
+            nc.scalar.activation(pairs[t][:], larger[:], ACT.Identity, bias=shift[:, t : t + 1])
+            if t >= PACK - GROUPS:
+                round_w2(t - (PACK - GROUPS))
+        for g in range(GROUPS):
+            quantize_w2(g)
+
+        y_codes = keep.tile([P, GROUPS, KEPT], U32, align_bytes=64)
+        y_planes = keep.tile([P, KEPT], U8, align_bytes=64)
+        y_rows = out_0.rearrange("(g p t) m -> g p t m", g=GROUPS, t=PACK)
+        words_out = out_1.rearrange("g p m t -> p g (m t)").bitcast(I32)
+        per = BLOCK // 16
+        a2_rounded = {}
+        a2_packed = {}
+        y_rounded = {}
+
+        def pick(b):
+            cols = slice(BLOCK * b, BLOCK * (b + 1))
+            kept = ring2.tile([P, PACK, BLOCK], F32, name="kept")
+            for t in range(PACK):
+                nc.vector.tensor_tensor(
+                    kept[:, t, :], pairs[t][:].indirect(p3[:, per * b : per * (b + 1)]), listing[t][:, cols], ALU.mult
+                )
+            rounded = ring2.tile([P, BLOCK, PACK], BF16, name="a2_rounded", align_bytes=64)
+            nc.scalar.copy(
+                out=rounded[:].rearrange("p (c i) t -> p c t i", i=4),
+                in_=kept[:].rearrange("p t (c i) -> p c t i", i=4),
+            )
+            a2_rounded[b] = rounded
+
+        def multiply(b):
+            cols = slice(BLOCK * b, BLOCK * (b + 1))
+            codes = ring2.tile([P, BLOCK], U32, name="a2_codes", align_bytes=64)
+            plane = ring2.tile([P, BLOCK], U8, name="a2_plane", align_bytes=64)
+            nc.vector.quantize_mx(
+                out=codes[:].bitcast(FP8X4), scales=plane[:], in_=a2_rounded[b][:].rearrange("p m t -> p (m t)")
+            )
+            for g in range(GROUPS):
+                bank = psum.tile([P, PACK, BLOCK], F32, name="bank")
+                for t in range(PACK):
+                    nc.tensor.matmul_mx(
+                        out=bank[:, t, :],
+                        lhsT=w2_codes[:, g, t, :].bitcast(FP8X4),
+                        lhsT_scale=w2_planes[:, g, t, :],
+                        rhs=codes[:].bitcast(FP8X4),
+                        rhs_scale=plane[:],
+                        start=True,
+                        stop=True,
+                    )
+                rounded = ring2.tile([P, BLOCK, PACK], BF16, name=f"y_rounded{g}", align_bytes=64)
+                y = ring3.tile([P, PACK, BLOCK], F32, name=f"y{g}")
+                if g == 0:
+                    nc.scalar.copy(out=rounded[:], in_=bank[:].rearrange("p t m -> p m t"))
+                    nc.scalar.copy(out=y[:], in_=bank[:])
+                else:
+                    nc.vector.tensor_copy(out=rounded[:], in_=bank[:].rearrange("p t m -> p m t"))
+                    nc.scalar.copy(out=y[:], in_=bank[:])
+                nc.sync.dma_start(out=y_rows[g, :, :, cols], in_=y[:])
+                y_rounded[b, g] = rounded
+
+        def emit_planes(b):
+            cols = slice(BLOCK * b, BLOCK * (b + 1))
+            for g in reversed(range(GROUPS)):
+                nc.vector.quantize_mx(
+                    out=y_codes[:, g, cols].bitcast(FP8X4),
+                    scales=y_planes[PACK * g : P, cols],
+                    in_=y_rounded[b, g][:].rearrange("p m t -> p (m t)"),
+                )
+            nc.sync.dma_start(out=words_out[:, :, cols], in_=y_codes[:, :, cols].bitcast(I32))
+
+        for step in range(BLOCKS + 2):
+            if step < BLOCKS:
+                pick(step)
+            if 1 <= step <= BLOCKS:
+                multiply(step - 1)
+            if step >= 2:
+                emit_planes(step - 2)
+        for q in range(4):
+            nc.sync.dma_start(
+                out=out_2[:, PACK * q : PACK * (q + 1), :].bitcast(I32),
+                in_=y_planes[QUAD * q : QUAD * q + GROUPS * PACK, :].bitcast(I32),
+            )

@@ -25,8 +25,7 @@ CHUNKS = S // CHUNK
 BLOCK = 128
 BLOCKS = KEPT // BLOCK
 QUAD = 32
-PARKED = QUAD - PASSES * PACK
-SPAN = 3 * QUAD + PACK
+PARKED = P - QUAD
 
 
 def tile_list_stolen_view_features_kernel(
@@ -38,6 +37,7 @@ def tile_list_stolen_view_features_kernel(
         keep = ctx.enter_context(tc.tile_pool(name="keep", bufs=1))
         ring2 = ctx.enter_context(tc.tile_pool(name="ring2", bufs=2))
         ring3 = ctx.enter_context(tc.tile_pool(name="ring3", bufs=3))
+        shared = ctx.enter_context(tc.tile_pool(name="shared", bufs=1))
         psum = ctx.enter_context(tc.psum_pool(name="psum", bufs=8))
 
         def load_list(src, name):
@@ -47,14 +47,11 @@ def tile_list_stolen_view_features_kernel(
 
         idx = load_list(offs, "idx")
         table_scales = keep.tile([P, T], U8, align_bytes=64)
-        for q in range(4):
-            nc.sync.dma_start(
-                out=table_scales[QUAD * q + PARKED : QUAD * (q + 1), :].bitcast(I32),
-                in_=tab_scales[:, PACK * q : PACK * (q + 1), :].bitcast(I32),
-            )
-        for q in range(4):
-            eng = nc.vector if q % 2 == 0 else nc.gpsimd
-            eng.memset(table_scales[QUAD * q : QUAD * q + PARKED, :].bitcast(I32), 0)
+        nc.sync.dma_start(
+            out=table_scales[PARKED:P, :].bitcast(I32), in_=tab_scales.rearrange("a q c -> q a c").bitcast(I32)
+        )
+        nc.vector.memset(table_scales[0:64, :].bitcast(I32), 0)
+        nc.vector.memset(table_scales[64:PARKED, :].bitcast(I32), 0)
 
         table_words = [keep.tile([P, T], U32, name=f"table_words{a}", align_bytes=64) for a in range(PASSES)]
 
@@ -63,50 +60,65 @@ def tile_list_stolen_view_features_kernel(
                 out=table_words[a][:].bitcast(I32), in_=tab_words[a].rearrange("p n t -> p (n t)").bitcast(I32)
             )
 
+        w4_scales_raw = keep.tile([P, PASSES, H], U8, align_bytes=64)
+        for q in range(4):
+            nc.sync.dma_start(
+                out=w4_scales_raw[QUAD * q : QUAD * q + PACK, :, :].bitcast(I32),
+                in_=w4_scales[:, PACK * q : PACK * (q + 1), :].rearrange("a r c -> r a c").bitcast(I32),
+            )
         load_table_words(0)
+        w4_raw = shared.tile([P, PASSES, 2 * H], U8, offset=4 * S - 2 * H)
+        nc.sync.dma_start(out=w4_raw[:].bitcast(I32), in_=w4_words.rearrange("a p c -> p a c").bitcast(I32))
+        load_table_words(1)
         p1 = load_list(pos1, "p1")
         p2 = load_list(pos2, "p2")
         p4 = load_list(pos4, "p4")
         p3 = load_list(pos3, "p3")
-        w4_raw = keep.tile([P, PASSES, 2 * H], U8, align_bytes=64)
-        nc.sync.dma_start(out=w4_raw[:].bitcast(I32), in_=w4_words.rearrange("a p c -> p a c").bitcast(I32))
-        load_table_words(1)
-        gm_rows = gm.rearrange("(p t) j -> p t j", t=PACK)
-        gains = [keep.tile([P, S], F32, name=f"gains{t}") for t in range(PACK)]
+        gm_rows = gm.rearrange("(b t i) j -> t b i j", t=PACK, i=PACK)
+        gains = {}
+
+        def load_gains(t):
+            if t % 2 == 0:
+                gains[t] = keep.tile([P, S], F32, name="gains_even")
+            else:
+                gains[t] = shared.tile([P, S], F32, name=f"gains_odd{t}", offset=0)
+            nc.sync.dma_start(out=gains[t][:], in_=gm_rows[t])
+
+        load_gains(0)
+        shift = [keep.tile([P, 1], F32, name=f"shift{t}") for t in range(PACK)]
+        slope = [keep.tile([P, 1], F32, name=f"slope{t}") for t in range(PACK)]
         for t in range(PACK):
-            nc.sync.dma_start(out=gains[t][:], in_=gm_rows[:, t, :])
-        w2_raw = keep.tile([P, PACK, N], F32)
-        nc.sync.dma_start(out=w2_raw[:], in_=w2.rearrange("(p j) n -> p j n", j=PACK))
-
-        w4_scales_raw = keep.tile([P, PASSES, H], U8, align_bytes=64)
-        nc.gpsimd.memset(w4_scales_raw[:].bitcast(I32), 0)
-        for q in range(4):
-            nc.gpsimd.dma_start(
-                out=w4_scales_raw[QUAD * q : QUAD * q + PACK, :, :].bitcast(I32),
-                in_=w4_scales[:, PACK * q : PACK * (q + 1), :].rearrange("a r c -> r a c").bitcast(I32),
-            )
-        shift = keep.tile([P, PACK], F32)
-        nc.gpsimd.dma_start(out=shift[:], in_=d.rearrange("(p t) -> p t", t=PACK))
-        slope = keep.tile([P, PACK], F32)
-        nc.gpsimd.dma_start(out=slope[:], in_=sv.rearrange("(p t) -> p t", t=PACK))
-
-        w4_codes = keep.tile([P, PASSES, PACK, 2 * P], U8, align_bytes=64)
-        nc.scalar.copy(
-            out=w4_codes[:].bitcast(U16),
-            in_=w4_raw[:].bitcast(U16).rearrange("p a (m t) -> p a t m", t=PACK),
-        )
-        w4_planes = keep.tile([P, PASSES, PACK, P], U8, align_bytes=64)
-        nc.gpsimd.tensor_copy(out=w4_planes[:], in_=w4_scales_raw[:].rearrange("p a (m t) -> p a t m", t=PACK))
+            nc.gpsimd.dma_start(out=slope[t][:], in_=sv.rearrange("(b t i o) -> t b i o", t=PACK, i=PACK, o=1)[t])
+            nc.gpsimd.dma_start(out=shift[t][:], in_=d.rearrange("(b t i o) -> t b i o", t=PACK, i=PACK, o=1)[t])
 
         picked_scales = keep.tile([P, S], U8, align_bytes=64)
         nc.vector.tensor_copy(picked_scales[:], table_scales[:].indirect(idx[:]))
         v_planes = keep.tile([P, PASSES, S], U8, align_bytes=64)
-        nc.gpsimd.memset(v_planes[:].bitcast(I32), 0)
-        for a in range(PASSES):
-            first = PARKED + PACK * a
+        for q in range(4):
+            first = PARKED + PASSES * PACK * q
             nc.scalar.dma_start(
-                out=v_planes[0:SPAN, a, :].bitcast(I32), in_=picked_scales[first : first + SPAN, :].bitcast(I32)
+                out=v_planes[QUAD * q : QUAD * q + PACK, :, :].bitcast(I32),
+                in_=picked_scales[first : first + PASSES * PACK, :].bitcast(I32),
             )
+
+        w4_planes = keep.tile([P, PASSES, PACK, P], U8, align_bytes=64)
+        for q in range(4):
+            rows = slice(QUAD * q, QUAD * q + PACK)
+            nc.scalar.copy(
+                out=w4_planes[rows].bitcast(U32),
+                in_=w4_scales_raw[rows].bitcast(U32).rearrange("p a (b t) -> p a t b", t=PACK),
+            )
+        w4_codes = keep.tile([P, PASSES, PACK, 2 * P], U8, align_bytes=64)
+        nc.scalar.copy(
+            out=w4_codes[:].bitcast(U32).rearrange("p a t (b w) -> p a t b w", w=2),
+            in_=w4_raw[:].bitcast(U32).rearrange("p a (b t w) -> p a t b w", t=PACK, w=2),
+        )
+        load_gains(1)
+        w2_raw = shared.tile([P, PACK, N], F32, offset=4 * S)
+        w2_rows = w2.rearrange("(b j i) n -> j b i n", j=PACK, i=PACK)
+        for j in range(PACK):
+            nc.sync.dma_start(out=w2_raw[:, j, :], in_=w2_rows[j])
+
         v_first = keep.tile([P, S], U32, align_bytes=64)
         nc.vector.tensor_copy(v_first[:], table_words[0][:].indirect(idx[:]))
         v_second = [keep.tile([P, CHUNK], U32, name=f"v_second{c}", align_bytes=64) for c in range(CHUNKS)]
@@ -119,10 +131,9 @@ def tile_list_stolen_view_features_kernel(
         w2_rounded = [keep.tile([P, PACK, P, PACK], BF16, name=f"w2_rounded{g}", align_bytes=64) for g in range(GROUPS)]
 
         def round_w2(g):
-            nc.scalar.copy(
-                out=w2_rounded[g][:].rearrange("p t m j -> p m j t"),
-                in_=w2_raw[:, :, 512 * g : 512 * (g + 1)].rearrange("p j (m t) -> p m j t", t=PACK),
-            )
+            dealt = w2_raw[:, :, 512 * g : 512 * (g + 1)].rearrange("p j (m t) -> p t m j", t=PACK)
+            for t in range(PACK):
+                nc.scalar.copy(out=w2_rounded[g][:, t], in_=dealt[:, t])
 
         def quantize_w2(g):
             nc.vector.quantize_mx(
@@ -133,8 +144,10 @@ def tile_list_stolen_view_features_kernel(
 
         pairs = [keep.tile([P, PAIRS], F32, name=f"pairs{t}") for t in range(PACK)]
         listing = [keep.tile([P, KEPT], F32, name=f"listing{t}") for t in range(PACK)]
-        for t in range(PACK):
-            views = ring3.tile([P, S], F32, name="views")
+        views = {}
+
+        def first_product(t):
+            views[t] = ring2.tile([P, S], F32, name="views")
             for c in range(CHUNKS):
                 cols = slice(CHUNK * c, CHUNK * (c + 1))
                 bank = psum.tile([P, CHUNK], F32, name="bank")
@@ -149,21 +162,34 @@ def tile_list_stolen_view_features_kernel(
                         start=(a == 0),
                         stop=(a == PASSES - 1),
                     )
-                nc.vector.tensor_tensor(views[:, cols], bank[:], gains[t][:, cols], ALU.mult)
-            left = keep.tile([P, PAIRS], F32, name="left")
-            right = keep.tile([P, PAIRS], F32, name="right")
-            nc.vector.tensor_copy(left[:], views[:].indirect(p1[:]))
-            nc.vector.tensor_copy(right[:], views[:].indirect(p2[:]))
+                nc.vector.tensor_tensor(views[t][:, cols], bank[:], gains[t][:, cols], ALU.mult)
+            if t + 2 < PACK:
+                load_gains(t + 2)
+
+        def look(t):
             listed = ring2.tile([P, KEPT], F32, name="listed")
-            nc.vector.tensor_copy(listed[:], views[:].indirect(p4[:]))
+            nc.vector.tensor_copy(listed[:], views[t][:].indirect(p4[:]))
+            nc.scalar.activation(listing[t][:], listed[:], ACT.Tanh, scale=slope[t][:])
+
+        first_product(0)
+        for t in range(PACK):
+            left = ring2.tile([P, PAIRS], F32, name="left")
+            right = ring2.tile([P, PAIRS], F32, name="right")
+            nc.vector.tensor_copy(left[:], views[t][:].indirect(p1[:]))
+            nc.vector.tensor_copy(right[:], views[t][:].indirect(p2[:]))
+            if t + 1 < PACK:
+                look(t)
+                first_product(t + 1)
+            else:
+                for g in range(GROUPS):
+                    quantize_w2(g)
             larger = ring2.tile([P, PAIRS], F32, name="larger")
             nc.vector.tensor_tensor(larger[:], left[:], right[:], ALU.max)
-            nc.scalar.activation(listing[t][:], listed[:], ACT.Tanh, scale=slope[:, t : t + 1])
-            nc.scalar.activation(pairs[t][:], larger[:], ACT.Identity, bias=shift[:, t : t + 1])
-            if t >= PACK - GROUPS:
-                round_w2(t - (PACK - GROUPS))
-        for g in range(GROUPS):
-            quantize_w2(g)
+            nc.scalar.activation(pairs[t][:], larger[:], ACT.Identity, bias=shift[t][:])
+            if t + 1 == PACK:
+                look(t)
+            if t < GROUPS:
+                round_w2(t)
 
         y_codes = keep.tile([P, GROUPS, KEPT], U32, align_bytes=64)
         y_planes = keep.tile([P, KEPT], U8, align_bytes=64)

@@ -126,7 +126,6 @@ def tile_list_stolen_view_features_kernel(
         for c in range(CHUNKS):
             nc.vector.tensor_copy(v_second[c][:], table_words[1][:].indirect(idx[:, per * c : per * (c + 1)]))
 
-        w2_codes = keep.tile([P, GROUPS, PACK, P], U32, align_bytes=64)
         w2_planes = keep.tile([P, GROUPS, PACK, P], U8, align_bytes=64)
         w2_rounded = [keep.tile([P, PACK, P, PACK], BF16, name=f"w2_rounded{g}", align_bytes=64) for g in range(GROUPS)]
 
@@ -135,7 +134,7 @@ def tile_list_stolen_view_features_kernel(
             for t in range(PACK):
                 nc.scalar.copy(out=w2_rounded[g][:, t], in_=dealt[:, t])
 
-        def quantize_w2(g):
+        def quantize_w2(g, w2_codes):
             nc.vector.quantize_mx(
                 out=w2_codes[:, g].rearrange("p t m -> p (t m)").bitcast(FP8X4),
                 scales=w2_planes[:, g].rearrange("p t m -> p (t m)"),
@@ -147,7 +146,7 @@ def tile_list_stolen_view_features_kernel(
         views = {}
 
         def first_product(t):
-            views[t] = ring2.tile([P, S], F32, name="views")
+            views[t] = keep.tile([P, S], F32, name=f"views{t}")
             for c in range(CHUNKS):
                 cols = slice(CHUNK * c, CHUNK * (c + 1))
                 bank = psum.tile([P, CHUNK], F32, name="bank")
@@ -162,7 +161,11 @@ def tile_list_stolen_view_features_kernel(
                         start=(a == 0),
                         stop=(a == PASSES - 1),
                     )
-                nc.vector.tensor_tensor(views[t][:, cols], bank[:], gains[t][:, cols], ALU.mult)
+                if t == 0:
+                    nc.vector.tensor_tensor(views[t][:, cols], bank[:], gains[t][:, cols], ALU.mult)
+                else:
+                    nc.scalar.copy(out=views[t][:, cols], in_=bank[:])
+                    nc.gpsimd.tensor_tensor(views[t][:, cols], views[t][:, cols], gains[t][:, cols], ALU.mult)
             if t + 2 < PACK:
                 load_gains(t + 2)
 
@@ -171,18 +174,19 @@ def tile_list_stolen_view_features_kernel(
             nc.vector.tensor_copy(listed[:], views[t][:].indirect(p4[:]))
             nc.scalar.activation(listing[t][:], listed[:], ACT.Tanh, scale=slope[t][:])
 
-        first_product(0)
         for t in range(PACK):
-            left = ring2.tile([P, PAIRS], F32, name="left")
+            first_product(t)
+        for t in range(PACK):
+            left = ring2.tile([P, PAIRS], F32, name="left", align_bytes=64)
             right = ring2.tile([P, PAIRS], F32, name="right")
             nc.vector.tensor_copy(left[:], views[t][:].indirect(p1[:]))
             nc.vector.tensor_copy(right[:], views[t][:].indirect(p2[:]))
             if t + 1 < PACK:
                 look(t)
-                first_product(t + 1)
             else:
+                w2_codes = ring2.tile([P, GROUPS, PACK, P], U32, name="left", align_bytes=64)
                 for g in range(GROUPS):
-                    quantize_w2(g)
+                    quantize_w2(g, w2_codes)
             larger = ring2.tile([P, PAIRS], F32, name="larger")
             nc.vector.tensor_tensor(larger[:], left[:], right[:], ALU.max)
             nc.scalar.activation(pairs[t][:], larger[:], ACT.Identity, bias=shift[t][:])

@@ -18,14 +18,19 @@ ACT = mybir.ActivationFunctionType
 
 P = 128
 PACK = 4
+QUAD = 32
+QUADS = P // QUAD
+PER_COLUMN = 16
 PASSES = K // (P * PACK)
 GROUPS = N // (P * PACK)
 CHUNK = 512
 CHUNKS = S // CHUNK
 BLOCK = 128
 BLOCKS = KEPT // BLOCK
-QUAD = 32
 PARKED = P - QUAD
+GAINS_BYTES = 4 * S
+PAIRS_BYTES = 4 * PAIRS
+LATE = 1
 
 
 def tile_list_stolen_view_features_kernel(
@@ -35,10 +40,15 @@ def tile_list_stolen_view_features_kernel(
     with ExitStack() as ctx:
         lists = ctx.enter_context(tc.tile_pool(name="lists", bufs=1))
         keep = ctx.enter_context(tc.tile_pool(name="keep", bufs=1))
+        loads = ctx.enter_context(tc.tile_pool(name="loads", bufs=1))
+        lefts = ctx.enter_context(tc.tile_pool(name="lefts", bufs=1))
         ring2 = ctx.enter_context(tc.tile_pool(name="ring2", bufs=2))
         ring3 = ctx.enter_context(tc.tile_pool(name="ring3", bufs=3))
-        shared = ctx.enter_context(tc.tile_pool(name="shared", bufs=1))
         psum = ctx.enter_context(tc.psum_pool(name="psum", bufs=8))
+
+        gains_at = {0: 0, 2: 0, 1: GAINS_BYTES, 3: GAINS_BYTES}
+        w2_raw_at = 2 * GAINS_BYTES
+        w4_raw_at = w2_raw_at - 2 * H
 
         def load_list(src, name):
             held = lists.tile(list(src.shape), U16, name=name)
@@ -50,8 +60,15 @@ def tile_list_stolen_view_features_kernel(
         nc.sync.dma_start(
             out=table_scales[PARKED:P, :].bitcast(I32), in_=tab_scales.rearrange("a q c -> q a c").bitcast(I32)
         )
-        nc.vector.memset(table_scales[0:64, :].bitcast(I32), 0)
-        nc.vector.memset(table_scales[64:PARKED, :].bitcast(I32), 0)
+        nc.vector.memset(table_scales[0 : 2 * QUAD, :].bitcast(I32), 0)
+        nc.vector.memset(table_scales[2 * QUAD : PARKED, :].bitcast(I32), 0)
+
+        w4_scales_raw = keep.tile([P, PASSES, H], U8, align_bytes=64)
+        for q in range(QUADS):
+            nc.sync.dma_start(
+                out=w4_scales_raw[QUAD * q : QUAD * q + PACK, :, :].bitcast(I32),
+                in_=w4_scales[:, PACK * q : PACK * (q + 1), :].rearrange("a r c -> r a c").bitcast(I32),
+            )
 
         table_words = [keep.tile([P, T], U32, name=f"table_words{a}", align_bytes=64) for a in range(PASSES)]
 
@@ -60,33 +77,25 @@ def tile_list_stolen_view_features_kernel(
                 out=table_words[a][:].bitcast(I32), in_=tab_words[a].rearrange("p n t -> p (n t)").bitcast(I32)
             )
 
-        w4_scales_raw = keep.tile([P, PASSES, H], U8, align_bytes=64)
-        for q in range(4):
-            nc.sync.dma_start(
-                out=w4_scales_raw[QUAD * q : QUAD * q + PACK, :, :].bitcast(I32),
-                in_=w4_scales[:, PACK * q : PACK * (q + 1), :].rearrange("a r c -> r a c").bitcast(I32),
-            )
         load_table_words(0)
-        w4_raw = shared.tile([P, PASSES, 2 * H], U8, offset=4 * S - 2 * H)
+        w4_raw = loads.tile([P, PASSES, 2 * H], U8, offset=w4_raw_at)
         nc.sync.dma_start(out=w4_raw[:].bitcast(I32), in_=w4_words.rearrange("a p c -> p a c").bitcast(I32))
         load_table_words(1)
         p1 = load_list(pos1, "p1")
         p2 = load_list(pos2, "p2")
         p4 = load_list(pos4, "p4")
         p3 = load_list(pos3, "p3")
+
         gm_rows = gm.rearrange("(b t i) j -> t b i j", t=PACK, i=PACK)
         gains = {}
 
         def load_gains(t):
-            if t % 2 == 0:
-                gains[t] = keep.tile([P, S], F32, name="gains_even")
-            else:
-                gains[t] = shared.tile([P, S], F32, name=f"gains_odd{t}", offset=0)
+            gains[t] = loads.tile([P, S], F32, name=f"gains{t}", offset=gains_at[t])
             nc.sync.dma_start(out=gains[t][:], in_=gm_rows[t])
 
         load_gains(0)
-        shift = [keep.tile([P, 1], F32, name=f"shift{t}") for t in range(PACK)]
         slope = [keep.tile([P, 1], F32, name=f"slope{t}") for t in range(PACK)]
+        shift = [keep.tile([P, 1], F32, name=f"shift{t}") for t in range(PACK)]
         for t in range(PACK):
             nc.gpsimd.dma_start(out=slope[t][:], in_=sv.rearrange("(b t i o) -> t b i o", t=PACK, i=PACK, o=1)[t])
             nc.gpsimd.dma_start(out=shift[t][:], in_=d.rearrange("(b t i o) -> t b i o", t=PACK, i=PACK, o=1)[t])
@@ -94,7 +103,7 @@ def tile_list_stolen_view_features_kernel(
         picked_scales = keep.tile([P, S], U8, align_bytes=64)
         nc.vector.tensor_copy(picked_scales[:], table_scales[:].indirect(idx[:]))
         v_planes = keep.tile([P, PASSES, S], U8, align_bytes=64)
-        for q in range(4):
+        for q in range(QUADS):
             first = PARKED + PASSES * PACK * q
             nc.scalar.dma_start(
                 out=v_planes[QUAD * q : QUAD * q + PACK, :, :].bitcast(I32),
@@ -102,7 +111,7 @@ def tile_list_stolen_view_features_kernel(
             )
 
         w4_planes = keep.tile([P, PASSES, PACK, P], U8, align_bytes=64)
-        for q in range(4):
+        for q in range(QUADS):
             rows = slice(QUAD * q, QUAD * q + PACK)
             nc.scalar.copy(
                 out=w4_planes[rows].bitcast(U32),
@@ -114,7 +123,7 @@ def tile_list_stolen_view_features_kernel(
             in_=w4_raw[:].bitcast(U32).rearrange("p a (b t w) -> p a t b w", t=PACK, w=2),
         )
         load_gains(1)
-        w2_raw = shared.tile([P, PACK, N], F32, offset=4 * S)
+        w2_raw = loads.tile([P, PACK, N], F32, offset=w2_raw_at)
         w2_rows = w2.rearrange("(b j i) n -> j b i n", j=PACK, i=PACK)
         for j in range(PACK):
             nc.sync.dma_start(out=w2_raw[:, j, :], in_=w2_rows[j])
@@ -122,35 +131,17 @@ def tile_list_stolen_view_features_kernel(
         v_first = keep.tile([P, S], U32, align_bytes=64)
         nc.vector.tensor_copy(v_first[:], table_words[0][:].indirect(idx[:]))
         v_second = [keep.tile([P, CHUNK], U32, name=f"v_second{c}", align_bytes=64) for c in range(CHUNKS)]
-        per = CHUNK // 16
+        span = CHUNK // PER_COLUMN
         for c in range(CHUNKS):
-            nc.vector.tensor_copy(v_second[c][:], table_words[1][:].indirect(idx[:, per * c : per * (c + 1)]))
+            nc.vector.tensor_copy(v_second[c][:], table_words[1][:].indirect(idx[:, span * c : span * (c + 1)]))
 
-        w2_planes = keep.tile([P, GROUPS, PACK, P], U8, align_bytes=64)
-        w2_rounded = [keep.tile([P, PACK, P, PACK], BF16, name=f"w2_rounded{g}", align_bytes=64) for g in range(GROUPS)]
-
-        def round_w2(g):
-            dealt = w2_raw[:, :, 512 * g : 512 * (g + 1)].rearrange("p j (m t) -> p t m j", t=PACK)
-            for t in range(PACK):
-                nc.scalar.copy(out=w2_rounded[g][:, t], in_=dealt[:, t])
-
-        def quantize_w2(g, w2_codes):
-            nc.vector.quantize_mx(
-                out=w2_codes[:, g].rearrange("p t m -> p (t m)").bitcast(FP8X4),
-                scales=w2_planes[:, g].rearrange("p t m -> p (t m)"),
-                in_=w2_rounded[g][:].rearrange("p t m j -> p (t m j)"),
-            )
-
-        pairs = [keep.tile([P, PAIRS], F32, name=f"pairs{t}") for t in range(PACK)]
-        listing = [keep.tile([P, KEPT], F32, name=f"listing{t}") for t in range(PACK)]
-        views = {}
+        views = [keep.tile([P, S], F32, name=f"views{t}") for t in range(PACK)]
 
         def first_product(t):
-            views[t] = keep.tile([P, S], F32, name=f"views{t}")
             for c in range(CHUNKS):
                 cols = slice(CHUNK * c, CHUNK * (c + 1))
                 bank = psum.tile([P, CHUNK], F32, name="bank")
-                for a in range(PASSES):
+                for a in reversed(range(PASSES)):
                     moving = v_first[:, cols] if a == 0 else v_second[c][:]
                     nc.tensor.matmul_mx(
                         out=bank[:],
@@ -158,99 +149,110 @@ def tile_list_stolen_view_features_kernel(
                         lhsT_scale=w4_planes[:, a, t, :],
                         rhs=moving.bitcast(FP8X4),
                         rhs_scale=v_planes[:, a, cols],
-                        start=(a == 0),
-                        stop=(a == PASSES - 1),
+                        start=(a == PASSES - 1),
+                        stop=(a == 0),
                     )
                 if t == 0:
                     nc.vector.tensor_tensor(views[t][:, cols], bank[:], gains[t][:, cols], ALU.mult)
                 else:
                     nc.scalar.copy(out=views[t][:, cols], in_=bank[:])
                     nc.gpsimd.tensor_tensor(views[t][:, cols], views[t][:, cols], gains[t][:, cols], ALU.mult)
-            if t + 2 < PACK:
-                load_gains(t + 2)
-
-        def look(t):
-            listed = ring2.tile([P, KEPT], F32, name="listed")
-            nc.vector.tensor_copy(listed[:], views[t][:].indirect(p4[:]))
-            nc.scalar.activation(listing[t][:], listed[:], ACT.Tanh, scale=slope[t][:])
 
         for t in range(PACK):
             first_product(t)
+            if t + 2 < PACK:
+                load_gains(t + 2)
+
+        w2_rounded = [keep.tile([P, PACK, P, PACK], BF16, name=f"w2_rounded{g}", align_bytes=64) for g in range(GROUPS)]
+
+        def round_w2(g):
+            dealt = w2_raw[:].rearrange("p j (g m t) -> p g t m j", g=GROUPS, t=PACK)
+            for t in range(PACK):
+                nc.scalar.copy(out=w2_rounded[g][:, t], in_=dealt[:, g, t])
+
+        pairs = [keep.tile([P, PAIRS], F32, name=f"pairs{t}") for t in range(PACK)]
+        listing = [keep.tile([P, KEPT], F32, name=f"listing{t}") for t in range(PACK)]
         for t in range(PACK):
-            left = ring2.tile([P, PAIRS], F32, name="left", align_bytes=64)
+            left = lefts.tile([P, PAIRS], F32, name=f"left{t}", align_bytes=64, offset=PAIRS_BYTES * (t % 2))
             right = ring2.tile([P, PAIRS], F32, name="right")
+            listed = ring2.tile([P, KEPT], F32, name="listed")
+            larger = ring2.tile([P, PAIRS], F32, name="larger")
             nc.vector.tensor_copy(left[:], views[t][:].indirect(p1[:]))
             nc.vector.tensor_copy(right[:], views[t][:].indirect(p2[:]))
-            if t + 1 < PACK:
-                look(t)
-            else:
-                w2_codes = ring2.tile([P, GROUPS, PACK, P], U32, name="left", align_bytes=64)
-                for g in range(GROUPS):
-                    quantize_w2(g, w2_codes)
-            larger = ring2.tile([P, PAIRS], F32, name="larger")
+            nc.vector.tensor_copy(listed[:], views[t][:].indirect(p4[:]))
             nc.vector.tensor_tensor(larger[:], left[:], right[:], ALU.max)
+            nc.scalar.activation(listing[t][:], listed[:], ACT.Tanh, scale=slope[t][:])
             nc.scalar.activation(pairs[t][:], larger[:], ACT.Identity, bias=shift[t][:])
-            if t + 1 == PACK:
-                look(t)
             if t < GROUPS:
                 round_w2(t)
+
+        w2_codes = lefts.tile([P, GROUPS, PACK, P], U32, align_bytes=64, offset=PAIRS_BYTES * ((PACK - 1) % 2))
+        w2_planes = keep.tile([P, GROUPS, PACK, P], U8, align_bytes=64)
+        for g in range(GROUPS):
+            nc.vector.quantize_mx(
+                out=w2_codes[:, g].rearrange("p t m -> p (t m)").bitcast(FP8X4),
+                scales=w2_planes[:, g].rearrange("p t m -> p (t m)"),
+                in_=w2_rounded[g][:].rearrange("p t m j -> p (t m j)"),
+            )
 
         y_codes = keep.tile([P, GROUPS, KEPT], U32, align_bytes=64)
         y_planes = keep.tile([P, KEPT], U8, align_bytes=64)
         y_rows = out_0.rearrange("(g p t) m -> g p t m", g=GROUPS, t=PACK)
         words_out = out_1.rearrange("g p m t -> p g (m t)").bitcast(I32)
-        per = BLOCK // 16
         a2_rounded = {}
-        a2_packed = {}
         y_rounded = {}
+
+        def weave(copy, rounded, values):
+            copy(
+                out=rounded[:].rearrange("p (c i) t -> p c t i", i=PACK),
+                in_=values[:].rearrange("p t (c i) -> p c t i", i=PACK),
+            )
 
         def pick(b):
             cols = slice(BLOCK * b, BLOCK * (b + 1))
-            kept = ring2.tile([P, PACK, BLOCK], F32, name="kept")
+            entries = p3[:, BLOCK // PER_COLUMN * b : BLOCK // PER_COLUMN * (b + 1)]
+            a2 = ring2.tile([P, PACK, BLOCK], F32, name="a2")
             for t in range(PACK):
-                nc.vector.tensor_tensor(
-                    kept[:, t, :], pairs[t][:].indirect(p3[:, per * b : per * (b + 1)]), listing[t][:, cols], ALU.mult
-                )
-            rounded = ring2.tile([P, BLOCK, PACK], BF16, name="a2_rounded", align_bytes=64)
-            nc.scalar.copy(
-                out=rounded[:].rearrange("p (c i) t -> p c t i", i=4),
-                in_=kept[:].rearrange("p t (c i) -> p c t i", i=4),
-            )
-            a2_rounded[b] = rounded
+                nc.vector.tensor_tensor(a2[:, t, :], pairs[t][:].indirect(entries), listing[t][:, cols], ALU.mult)
+            a2_rounded[b] = ring2.tile([P, BLOCK, PACK], BF16, name="a2_rounded", align_bytes=64)
+            weave(nc.vector.tensor_copy if b == BLOCKS - 1 else nc.scalar.copy, a2_rounded[b], a2)
 
-        def multiply(b):
+        def second_product(b):
             cols = slice(BLOCK * b, BLOCK * (b + 1))
-            codes = ring2.tile([P, BLOCK], U32, name="a2_codes", align_bytes=64)
-            plane = ring2.tile([P, BLOCK], U8, name="a2_plane", align_bytes=64)
+            a2_codes = ring2.tile([P, BLOCK], U32, name="a2_codes", align_bytes=64)
+            a2_plane = ring2.tile([P, BLOCK], U8, name="a2_plane", align_bytes=64)
             nc.vector.quantize_mx(
-                out=codes[:].bitcast(FP8X4), scales=plane[:], in_=a2_rounded[b][:].rearrange("p m t -> p (m t)")
+                out=a2_codes[:].bitcast(FP8X4),
+                scales=a2_plane[:],
+                in_=a2_rounded[b][:].rearrange("p m t -> p (m t)"),
             )
-            for g in range(GROUPS):
-                bank = psum.tile([P, PACK, BLOCK], F32, name="bank")
+            banks = {}
+            y = {}
+            for g in reversed(range(GROUPS)):
+                banks[g] = psum.tile([P, PACK, BLOCK], F32, name="bank")
                 for t in range(PACK):
                     nc.tensor.matmul_mx(
-                        out=bank[:, t, :],
+                        out=banks[g][:, t, :],
                         lhsT=w2_codes[:, g, t, :].bitcast(FP8X4),
                         lhsT_scale=w2_planes[:, g, t, :],
-                        rhs=codes[:].bitcast(FP8X4),
-                        rhs_scale=plane[:],
+                        rhs=a2_codes[:].bitcast(FP8X4),
+                        rhs_scale=a2_plane[:],
                         start=True,
                         stop=True,
                     )
-                rounded = ring2.tile([P, BLOCK, PACK], BF16, name=f"y_rounded{g}", align_bytes=64)
-                y = ring3.tile([P, PACK, BLOCK], F32, name=f"y{g}")
-                if g == 0:
-                    nc.scalar.copy(out=rounded[:], in_=bank[:].rearrange("p t m -> p m t"))
-                    nc.scalar.copy(out=y[:], in_=bank[:])
-                else:
-                    nc.vector.tensor_copy(out=rounded[:], in_=bank[:].rearrange("p t m -> p m t"))
-                    nc.scalar.copy(out=y[:], in_=bank[:])
-                nc.sync.dma_start(out=y_rows[g, :, :, cols], in_=y[:])
-                y_rounded[b, g] = rounded
+                y[g] = ring3.tile([P, PACK, BLOCK], F32, name=f"y{g}")
+                y_rounded[b, g] = ring2.tile([P, BLOCK, PACK], BF16, name=f"y_rounded{g}", align_bytes=64)
+            nc.scalar.copy(out=y[1][:], in_=banks[1][:])
+            nc.sync.dma_start(out=y_rows[1, :, :, cols], in_=y[1][:])
+            copy = nc.vector.tensor_copy if b >= BLOCKS - LATE else nc.scalar.copy
+            copy(out=y_rounded[b, 0][:], in_=banks[0][:].rearrange("p t m -> p m t"))
+            nc.scalar.copy(out=y[0][:], in_=banks[0][:])
+            nc.sync.dma_start(out=y_rows[0, :, :, cols], in_=y[0][:])
+            weave(nc.vector.tensor_copy, y_rounded[b, 1], y[1])
 
-        def emit_planes(b):
+        def store_words(b):
             cols = slice(BLOCK * b, BLOCK * (b + 1))
-            for g in reversed(range(GROUPS)):
+            for g in range(GROUPS):
                 nc.vector.quantize_mx(
                     out=y_codes[:, g, cols].bitcast(FP8X4),
                     scales=y_planes[PACK * g : P, cols],
@@ -262,10 +264,10 @@ def tile_list_stolen_view_features_kernel(
             if step < BLOCKS:
                 pick(step)
             if 1 <= step <= BLOCKS:
-                multiply(step - 1)
+                second_product(step - 1)
             if step >= 2:
-                emit_planes(step - 2)
-        for q in range(4):
+                store_words(step - 2)
+        for q in range(QUADS):
             nc.sync.dma_start(
                 out=out_2[:, PACK * q : PACK * (q + 1), :].bitcast(I32),
                 in_=y_planes[QUAD * q : QUAD * q + GROUPS * PACK, :].bitcast(I32),

from contextlib import ExitStack

import concourse.mybir as mybir

K, H, N, T, S, PAIRS, KEPT = 1024, 512, 1024, 4096, 2048, 1024, 512
FLOPS = 2 * (K * H * S + H * N * KEPT)

F32 = mybir.dt.float32
BF16 = mybir.dt.bfloat16
I32 = mybir.dt.int32
U32 = mybir.dt.uint32
U16 = mybir.dt.uint16
U8 = mybir.dt.uint8
FP8X4 = mybir.dt.float8_e4m3fn_x4
FP4X4 = mybir.dt.float4_e2m1fn_x4
ALU = mybir.AluOpType
ACT = mybir.ActivationFunctionType

P = 128
PACK = 4
QUAD = 32
QUADS = P // QUAD
PER_COLUMN = 16
PASSES = K // (P * PACK)
GROUPS = N // (P * PACK)
CHUNK = 512
CHUNKS = S // CHUNK
BLOCK = 128
BLOCKS = KEPT // BLOCK
PARKED = P - QUAD
GAINS_BYTES = 4 * S
PAIRS_BYTES = 4 * PAIRS
LATE = 1


def tile_list_stolen_view_features_kernel(
    tc, tab_words, tab_scales, offs, pos1, pos2, pos3, pos4, w4_words, w4_scales, gm, d, sv, w2, out_0, out_1, out_2
):
    nc = tc.nc
    with ExitStack() as ctx:
        lists = ctx.enter_context(tc.tile_pool(name="lists", bufs=1))
        keep = ctx.enter_context(tc.tile_pool(name="keep", bufs=1))
        loads = ctx.enter_context(tc.tile_pool(name="loads", bufs=1))
        lefts = ctx.enter_context(tc.tile_pool(name="lefts", bufs=1))
        ring2 = ctx.enter_context(tc.tile_pool(name="ring2", bufs=2))
        ring3 = ctx.enter_context(tc.tile_pool(name="ring3", bufs=3))
        psum = ctx.enter_context(tc.psum_pool(name="psum", bufs=8))

        gains_at = {0: 0, 2: 0, 1: GAINS_BYTES, 3: GAINS_BYTES}
        w2_raw_at = 2 * GAINS_BYTES
        w4_raw_at = w2_raw_at - 2 * H

        def load_list(src, name):
            held = lists.tile(list(src.shape), U16, name=name)
            nc.sync.dma_start(held[:], src)
            return held

        idx = load_list(offs, "idx")
        table_scales = keep.tile([P, T], U8, align_bytes=64)
        nc.sync.dma_start(
            out=table_scales[PARKED:P, :].bitcast(I32), in_=tab_scales.rearrange("a q c -> q a c").bitcast(I32)
        )
        nc.vector.memset(table_scales[0 : 2 * QUAD, :].bitcast(I32), 0)
        nc.vector.memset(table_scales[2 * QUAD : PARKED, :].bitcast(I32), 0)

        w4_scales_raw = keep.tile([P, PASSES, H], U8, align_bytes=64)
        for q in range(QUADS):
            nc.sync.dma_start(
                out=w4_scales_raw[QUAD * q : QUAD * q + PACK, :, :].bitcast(I32),
                in_=w4_scales[:, PACK * q : PACK * (q + 1), :].rearrange("a r c -> r a c").bitcast(I32),
            )

        table_words = [keep.tile([P, T], U32, name=f"table_words{a}", align_bytes=64) for a in range(PASSES)]

        def load_table_words(a):
            nc.sync.dma_start(
                out=table_words[a][:].bitcast(I32), in_=tab_words[a].rearrange("p n t -> p (n t)").bitcast(I32)
            )

        load_table_words(0)
        w4_raw = loads.tile([P, PASSES, 2 * H], U8, offset=w4_raw_at)
        nc.sync.dma_start(out=w4_raw[:].bitcast(I32), in_=w4_words.rearrange("a p c -> p a c").bitcast(I32))
        load_table_words(1)
        p1 = load_list(pos1, "p1")
        p2 = load_list(pos2, "p2")
        p4 = load_list(pos4, "p4")
        p3 = load_list(pos3, "p3")

        gm_rows = gm.rearrange("(b t i) j -> t b i j", t=PACK, i=PACK)
        gains = {}

        def load_gains(t):
            gains[t] = loads.tile([P, S], F32, name=f"gains{t}", offset=gains_at[t])
            nc.sync.dma_start(out=gains[t][:], in_=gm_rows[t])

        load_gains(0)
        slope = [keep.tile([P, 1], F32, name=f"slope{t}") for t in range(PACK)]
        shift = [keep.tile([P, 1], F32, name=f"shift{t}") for t in range(PACK)]
        for t in range(PACK):
            nc.gpsimd.dma_start(out=slope[t][:], in_=sv.rearrange("(b t i o) -> t b i o", t=PACK, i=PACK, o=1)[t])
            nc.gpsimd.dma_start(out=shift[t][:], in_=d.rearrange("(b t i o) -> t b i o", t=PACK, i=PACK, o=1)[t])

        picked_scales = keep.tile([P, S], U8, align_bytes=64)
        nc.vector.tensor_copy(picked_scales[:], table_scales[:].indirect(idx[:]))
        v_planes = keep.tile([P, PASSES, S], U8, align_bytes=64)
        for q in range(QUADS):
            first = PARKED + PASSES * PACK * q
            nc.scalar.dma_start(
                out=v_planes[QUAD * q : QUAD * q + PACK, :, :].bitcast(I32),
                in_=picked_scales[first : first + PASSES * PACK, :].bitcast(I32),
            )

        w4_planes = keep.tile([P, PASSES, PACK, P], U8, align_bytes=64)
        for q in range(QUADS):
            rows = slice(QUAD * q, QUAD * q + PACK)
            nc.scalar.copy(
                out=w4_planes[rows].bitcast(U32),
                in_=w4_scales_raw[rows].bitcast(U32).rearrange("p a (b t) -> p a t b", t=PACK),
            )
        w4_codes = keep.tile([P, PASSES, PACK, 2 * P], U8, align_bytes=64)
        nc.scalar.copy(
            out=w4_codes[:].bitcast(U32).rearrange("p a t (b w) -> p a t b w", w=2),
            in_=w4_raw[:].bitcast(U32).rearrange("p a (b t w) -> p a t b w", t=PACK, w=2),
        )
        load_gains(1)
        w2_raw = loads.tile([P, PACK, N], F32, offset=w2_raw_at)
        w2_rows = w2.rearrange("(b j i) n -> j b i n", j=PACK, i=PACK)
        for j in range(PACK):
            nc.sync.dma_start(out=w2_raw[:, j, :], in_=w2_rows[j])

        v_first = keep.tile([P, S], U32, align_bytes=64)
        nc.vector.tensor_copy(v_first[:], table_words[0][:].indirect(idx[:]))
        v_second = [keep.tile([P, CHUNK], U32, name=f"v_second{c}", align_bytes=64) for c in range(CHUNKS)]
        span = CHUNK // PER_COLUMN
        for c in range(CHUNKS):
            nc.vector.tensor_copy(v_second[c][:], table_words[1][:].indirect(idx[:, span * c : span * (c + 1)]))

        views = [keep.tile([P, S], F32, name=f"views{t}") for t in range(PACK)]

        def first_product(t):
            for c in range(CHUNKS):
                cols = slice(CHUNK * c, CHUNK * (c + 1))
                bank = psum.tile([P, CHUNK], F32, name="bank")
                for a in reversed(range(PASSES)):
                    moving = v_first[:, cols] if a == 0 else v_second[c][:]
                    nc.tensor.matmul_mx(
                        out=bank[:],
                        lhsT=w4_codes[:, a, t, :].bitcast(FP4X4),
                        lhsT_scale=w4_planes[:, a, t, :],
                        rhs=moving.bitcast(FP8X4),
                        rhs_scale=v_planes[:, a, cols],
                        start=(a == PASSES - 1),
                        stop=(a == 0),
                    )
                if t == 0:
                    nc.vector.tensor_tensor(views[t][:, cols], bank[:], gains[t][:, cols], ALU.mult)
                else:
                    nc.scalar.copy(out=views[t][:, cols], in_=bank[:])
                    nc.gpsimd.tensor_tensor(views[t][:, cols], views[t][:, cols], gains[t][:, cols], ALU.mult)

        for t in range(PACK):
            first_product(t)
            if t + 2 < PACK:
                load_gains(t + 2)

        w2_rounded = [keep.tile([P, PACK, P, PACK], BF16, name=f"w2_rounded{g}", align_bytes=64) for g in range(GROUPS)]

        def round_w2(g):
            dealt = w2_raw[:].rearrange("p j (g m t) -> p g t m j", g=GROUPS, t=PACK)
            for t in range(PACK):
                nc.scalar.copy(out=w2_rounded[g][:, t], in_=dealt[:, g, t])

        pairs = [keep.tile([P, PAIRS], F32, name=f"pairs{t}") for t in range(PACK)]
        listing = [keep.tile([P, KEPT], F32, name=f"listing{t}") for t in range(PACK)]
        for t in range(PACK):
            left = lefts.tile([P, PAIRS], F32, name=f"left{t}", align_bytes=64, offset=PAIRS_BYTES * (t % 2))
            right = ring2.tile([P, PAIRS], F32, name="right")
            listed = ring2.tile([P, KEPT], F32, name="listed")
            larger = ring2.tile([P, PAIRS], F32, name="larger")
            nc.vector.tensor_copy(left[:], views[t][:].indirect(p1[:]))
            nc.vector.tensor_copy(right[:], views[t][:].indirect(p2[:]))
            nc.vector.tensor_copy(listed[:], views[t][:].indirect(p4[:]))
            nc.vector.tensor_tensor(larger[:], left[:], right[:], ALU.max)
            nc.scalar.activation(listing[t][:], listed[:], ACT.Tanh, scale=slope[t][:])
            nc.scalar.activation(pairs[t][:], larger[:], ACT.Identity, bias=shift[t][:])
            if t < GROUPS:
                round_w2(t)

        w2_codes = lefts.tile([P, GROUPS, PACK, P], U32, align_bytes=64, offset=PAIRS_BYTES * ((PACK - 1) % 2))
        w2_planes = keep.tile([P, GROUPS, PACK, P], U8, align_bytes=64)
        for g in range(GROUPS):
            nc.vector.quantize_mx(
                out=w2_codes[:, g].rearrange("p t m -> p (t m)").bitcast(FP8X4),
                scales=w2_planes[:, g].rearrange("p t m -> p (t m)"),
                in_=w2_rounded[g][:].rearrange("p t m j -> p (t m j)"),
            )

        y_codes = keep.tile([P, GROUPS, KEPT], U32, align_bytes=64)
        y_planes = keep.tile([P, KEPT], U8, align_bytes=64)
        y_rows = out_0.rearrange("(g p t) m -> g p t m", g=GROUPS, t=PACK)
        words_out = out_1.rearrange("g p m t -> p g (m t)").bitcast(I32)
        a2_rounded = {}
        y_rounded = {}

        def weave(copy, rounded, values):
            copy(
                out=rounded[:].rearrange("p (c i) t -> p c t i", i=PACK),
                in_=values[:].rearrange("p t (c i) -> p c t i", i=PACK),
            )

        def pick(b):
            cols = slice(BLOCK * b, BLOCK * (b + 1))
            entries = p3[:, BLOCK // PER_COLUMN * b : BLOCK // PER_COLUMN * (b + 1)]
            a2 = ring2.tile([P, PACK, BLOCK], F32, name="a2")
            for t in range(PACK):
                nc.vector.tensor_tensor(a2[:, t, :], pairs[t][:].indirect(entries), listing[t][:, cols], ALU.mult)
            a2_rounded[b] = ring2.tile([P, BLOCK, PACK], BF16, name="a2_rounded", align_bytes=64)
            weave(nc.vector.tensor_copy if b == BLOCKS - 1 else nc.scalar.copy, a2_rounded[b], a2)

        def second_product(b):
            cols = slice(BLOCK * b, BLOCK * (b + 1))
            a2_codes = ring2.tile([P, BLOCK], U32, name="a2_codes", align_bytes=64)
            a2_plane = ring2.tile([P, BLOCK], U8, name="a2_plane", align_bytes=64)
            nc.vector.quantize_mx(
                out=a2_codes[:].bitcast(FP8X4),
                scales=a2_plane[:],
                in_=a2_rounded[b][:].rearrange("p m t -> p (m t)"),
            )
            banks = {}
            y = {}
            for g in reversed(range(GROUPS)):
                banks[g] = psum.tile([P, PACK, BLOCK], F32, name="bank")
                for t in range(PACK):
                    nc.tensor.matmul_mx(
                        out=banks[g][:, t, :],
                        lhsT=w2_codes[:, g, t, :].bitcast(FP8X4),
                        lhsT_scale=w2_planes[:, g, t, :],
                        rhs=a2_codes[:].bitcast(FP8X4),
                        rhs_scale=a2_plane[:],
                        start=True,
                        stop=True,
                    )
                y[g] = ring3.tile([P, PACK, BLOCK], F32, name=f"y{g}")
                y_rounded[b, g] = ring2.tile([P, BLOCK, PACK], BF16, name=f"y_rounded{g}", align_bytes=64)
            nc.scalar.copy(out=y[1][:], in_=banks[1][:])
            nc.sync.dma_start(out=y_rows[1, :, :, cols], in_=y[1][:])
            copy = nc.vector.tensor_copy if b >= BLOCKS - LATE else nc.scalar.copy
            copy(out=y_rounded[b, 0][:], in_=banks[0][:].rearrange("p t m -> p m t"))
            nc.scalar.copy(out=y[0][:], in_=banks[0][:])
            nc.sync.dma_start(out=y_rows[0, :, :, cols], in_=y[0][:])
            weave(nc.vector.tensor_copy, y_rounded[b, 1], y[1])

        def store_words(b):
            cols = slice(BLOCK * b, BLOCK * (b + 1))
            for g in range(GROUPS):
                nc.vector.quantize_mx(
                    out=y_codes[:, g, cols].bitcast(FP8X4),
                    scales=y_planes[PACK * g : P, cols],
                    in_=y_rounded[b, g][:].rearrange("p m t -> p (m t)"),
                )
            nc.sync.dma_start(out=words_out[:, :, cols], in_=y_codes[:, :, cols].bitcast(I32))

        for step in range(BLOCKS + 2):
            if step < BLOCKS:
                pick(step)
            if 1 <= step <= BLOCKS:
                second_product(step - 1)
            if step >= 2:
                store_words(step - 2)
        for q in range(QUADS):
            nc.sync.dma_start(
                out=out_2[:, PACK * q : PACK * (q + 1), :].bitcast(I32),
                in_=y_planes[QUAD * q : QUAD * q + GROUPS * PACK, :].bitcast(I32),
            )
